import numpy as np
CORES = [0,1,2,3,4,5,6,7]
N = 8
def setup_inputs(rng):
    return {"x": rng.standard_normal((N, 128, 128), dtype=np.float32)}
def reference(x):
    s = np.maximum.accumulate(x, axis=0)
    y = np.full(x.shape, np.nan, x.dtype)
    y[1:] = s[:-1]
    return {"y": y}

@@ -1,0 +1,40 @@
+from concourse.bass import DstId, RemoteDMATransfer
+
+SCRATCH = {
+    "xs": ("sbuf", [128, 128], "float32"),
+    "land": ("sbuf", [128, 128], "float32"),
+}
+SEMAPHORES = ["loaded", "arrived", "left", "stored"]
+
+
+def rank_program(g, core, T, topo):
+    rank = T.rank_of(core)
+    if rank is None:
+        return
+    last = len(T.cores) - 1
+
+    if rank < last:
+        g.sync.dma_start(T.xs[:], T.x[:]).then_inc(T.sem.loaded, 16)
+
+    if rank > 0:
+        g.scalar.wait_ge(T.sem.arrived, 16)
+        g.scalar.dma_start(T.y[:], T.land[:]).then_inc(T.sem.stored, 16)
+
+    if rank < last:
+        nxt = T.cores[rank + 1]
+        rid, pid, _se = topo.addr(nxt)
+        mask = topo.mask(core, nxt)
+        g.wait_ge(T.sem.loaded, 16)
+        if rank == 0:
+            g.remote_dma(T.land[:], T.xs[:], T.sem.arrived, T.sem.left, pid, rid, mask)
+        else:
+            g.wait_ge(T.sem.arrived, 16)
+            g.remote_dma_fused(
+                [RemoteDMATransfer(dst_ids=[DstId(rid=rid, pnc=pid)], dma_engine_mask=mask,
+                                   remote_sem=T.sem.arrived, srcs=[T.land[:], T.xs[:]], dsts=[T.land[:]],
+                                   alu_op=2)],
+                local_sem=T.sem.left)
+        g.wait_ge(T.sem.left, 16)
+
+    if rank > 0:
+        g.wait_ge(T.sem.stored, 16)

@@ -1,40 +1,120 @@
 from concourse.bass import DstId, RemoteDMATransfer
 
+N = 8
+S = 8
+WIDTH = 16
+PARTNER = {2: 1, 3: 2, 4: 3, 5: 0, 6: 1, 7: 0}
+
+
+def share_engines(weights):
+    even = 1
+    while 2 * even * len(weights) <= 16:
+        even *= 2
+    count = [even] * len(weights)
+    free = 16 - even * len(weights)
+    while True:
+        k = max(range(len(weights)), key=lambda j: (weights[j] / count[j], -j))
+        if count[k] > free:
+            break
+        free -= count[k]
+        count[k] *= 2
+    masks, bit = [], 0
+    for c in count:
+        masks.append(((1 << c) - 1) << bit)
+        bit += c
+    return count, masks
+
+
+def make_plan():
+    made = {c: [] for c in range(N)}
+    for s in range(S):
+        for r in range(1, N):
+            if r != s:
+                made[s].append((r, s))
+            elif r > 1:
+                made[PARTNER[r]].append((r, s))
+    needs = {c: sorted({(i, s) for (r, s) in made[c] for i in range(r) if i != c}) for c in range(N)}
+    direct = {s for (i, s) in needs[1] if i == 0}
+    for c in range(N):
+        made[c] = [(r, s) for (r, s) in made[c] if not (r == 1 and (s in direct or c == 0))]
+    needs[1] = sorted(needs[1] + [(0, 0)])
+
+    slot = {c: {} for c in range(N)}
+    sends = {i: [] for i in range(N)}
+    for c in range(N):
+        for (i, s) in needs[c]:
+            if not (c == 1 and i == 0):
+                slot[c][(i, s)] = len(slot[c])
+            sends[i].append((c, s))
+    step1, step2 = {}, {}
+    raw_sum, pre_sum, left_sum = [0] * N, [0] * N, [0] * N
+    for c in range(N):
+        step1[c], step2[c] = [], []
+        if sends[c]:
+            count, masks = share_engines([1] * len(sends[c]))
+            for (d, s), n, m in zip(sends[c], count, masks):
+                step1[c].append((d, s, n, m))
+                raw_sum[d] += n
+                left_sum[c] += n
+        count, masks = share_engines([r for (r, s) in made[c]])
+        for (r, s), n, m in zip(made[c], count, masks):
+            step2[c].append((r, s, n, m))
+            pre_sum[r] += n
+            left_sum[c] += n
+    return step1, step2, slot, raw_sum, pre_sum, left_sum
+
+
+PLAN = make_plan()
+
 SCRATCH = {
-    "xs": ("sbuf", [128, 128], "float32"),
-    "land": ("sbuf", [128, 128], "float32"),
+    "xs": ("dram", [S, 128, WIDTH], "float32"),
+    "land": ("dram", [S, 128, WIDTH], "float32"),
+    "raw": ("dram", [max(len(v) for v in PLAN[2].values()), 128, WIDTH], "float32"),
 }
-SEMAPHORES = ["loaded", "arrived", "left", "stored"]
+SEMAPHORES = ["loaded", "raw", "pre", "left", "stored"]
 
 
 def rank_program(g, core, T, topo):
-    rank = T.rank_of(core)
-    if rank is None:
+    me = T.rank_of(core)
+    if me is None:
         return
-    last = len(T.cores) - 1
+    step1, step2, slot, raw_sum, pre_sum, left_sum = PLAN
 
-    if rank < last:
+    def dst_id(rank):
+        rid, pid, _se = topo.addr(T.cores[rank])
+        return DstId(rid=rid, pnc=pid)
+
+    def place(holder, i, s):
+        if i == holder:
+            return T.xs[s]
+        if holder == 1 and i == 0:
+            return T.land[s]
+        return T.raw[slot[holder][(i, s)]]
+
+    if step1[me]:
         g.sync.dma_start(T.xs[:], T.x[:]).then_inc(T.sem.loaded, 16)
 
-    if rank > 0:
-        g.scalar.wait_ge(T.sem.arrived, 16)
+    if me > 0:
+        if me == 1:
+            g.scalar.wait_ge(T.sem.raw, raw_sum[me])
+        g.scalar.wait_ge(T.sem.pre, pre_sum[me])
         g.scalar.dma_start(T.y[:], T.land[:]).then_inc(T.sem.stored, 16)
 
-    if rank < last:
-        nxt = T.cores[rank + 1]
-        rid, pid, _se = topo.addr(nxt)
-        mask = topo.mask(core, nxt)
+    if step1[me]:
         g.wait_ge(T.sem.loaded, 16)
-        if rank == 0:
-            g.remote_dma(T.land[:], T.xs[:], T.sem.arrived, T.sem.left, pid, rid, mask)
-        else:
-            g.wait_ge(T.sem.arrived, 16)
-            g.remote_dma_fused(
-                [RemoteDMATransfer(dst_ids=[DstId(rid=rid, pnc=pid)], dma_engine_mask=mask,
-                                   remote_sem=T.sem.arrived, srcs=[T.land[:], T.xs[:]], dsts=[T.land[:]],
-                                   alu_op=2)],
-                local_sem=T.sem.left)
-        g.wait_ge(T.sem.left, 16)
+        g.remote_dma_fused(
+            [RemoteDMATransfer(dst_ids=[dst_id(d)], dma_engine_mask=m, remote_sem=T.sem.raw,
+                               srcs=[T.xs[s]], dsts=[place(d, me, s)], alu_op=0)
+             for (d, s, n, m) in step1[me]],
+            local_sem=T.sem.left)
+    g.wait_ge(T.sem.raw, raw_sum[me])
+    g.remote_dma_fused(
+        [RemoteDMATransfer(dst_ids=[dst_id(r)], dma_engine_mask=m, remote_sem=T.sem.pre,
+                           srcs=[place(me, i, s) for i in range(r)], dsts=[T.land[s]],
+                           alu_op=2 if r > 1 else 0)
+         for (r, s, n, m) in step2[me]],
+        local_sem=T.sem.left)
 
-    if rank > 0:
+    g.wait_ge(T.sem.left, left_sum[me])
+    if me > 0:
         g.wait_ge(T.sem.stored, 16)

from concourse.bass import DstId, RemoteDMATransfer

N = 8
S = 8
WIDTH = 16
PARTNER = {2: 1, 3: 2, 4: 3, 5: 0, 6: 1, 7: 0}


def share_engines(weights):
    even = 1
    while 2 * even * len(weights) <= 16:
        even *= 2
    count = [even] * len(weights)
    free = 16 - even * len(weights)
    while True:
        k = max(range(len(weights)), key=lambda j: (weights[j] / count[j], -j))
        if count[k] > free:
            break
        free -= count[k]
        count[k] *= 2
    masks, bit = [], 0
    for c in count:
        masks.append(((1 << c) - 1) << bit)
        bit += c
    return count, masks


def make_plan():
    made = {c: [] for c in range(N)}
    for s in range(S):
        for r in range(1, N):
            if r != s:
                made[s].append((r, s))
            elif r > 1:
                made[PARTNER[r]].append((r, s))
    needs = {c: sorted({(i, s) for (r, s) in made[c] for i in range(r) if i != c}) for c in range(N)}
    direct = {s for (i, s) in needs[1] if i == 0}
    for c in range(N):
        made[c] = [(r, s) for (r, s) in made[c] if not (r == 1 and (s in direct or c == 0))]
    needs[1] = sorted(needs[1] + [(0, 0)])

    slot = {c: {} for c in range(N)}
    sends = {i: [] for i in range(N)}
    for c in range(N):
        for (i, s) in needs[c]:
            if not (c == 1 and i == 0):
                slot[c][(i, s)] = len(slot[c])
            sends[i].append((c, s))
    step1, step2 = {}, {}
    raw_sum, pre_sum, left_sum = [0] * N, [0] * N, [0] * N
    for c in range(N):
        step1[c], step2[c] = [], []
        if sends[c]:
            count, masks = share_engines([1] * len(sends[c]))
            for (d, s), n, m in zip(sends[c], count, masks):
                step1[c].append((d, s, n, m))
                raw_sum[d] += n
                left_sum[c] += n
        count, masks = share_engines([r for (r, s) in made[c]])
        for (r, s), n, m in zip(made[c], count, masks):
            step2[c].append((r, s, n, m))
            pre_sum[r] += n
            left_sum[c] += n
    return step1, step2, slot, raw_sum, pre_sum, left_sum


PLAN = make_plan()

SCRATCH = {
    "xs": ("dram", [S, 128, WIDTH], "float32"),
    "land": ("dram", [S, 128, WIDTH], "float32"),
    "raw": ("dram", [max(len(v) for v in PLAN[2].values()), 128, WIDTH], "float32"),
}
SEMAPHORES = ["loaded", "raw", "pre", "left", "stored"]


def rank_program(g, core, T, topo):
    me = T.rank_of(core)
    if me is None:
        return
    step1, step2, slot, raw_sum, pre_sum, left_sum = PLAN

    def dst_id(rank):
        rid, pid, _se = topo.addr(T.cores[rank])
        return DstId(rid=rid, pnc=pid)

    def place(holder, i, s):
        if i == holder:
            return T.xs[s]
        if holder == 1 and i == 0:
            return T.land[s]
        return T.raw[slot[holder][(i, s)]]

    if step1[me]:
        g.sync.dma_start(T.xs[:], T.x[:]).then_inc(T.sem.loaded, 16)

    if me > 0:
        if me == 1:
            g.scalar.wait_ge(T.sem.raw, raw_sum[me])
        g.scalar.wait_ge(T.sem.pre, pre_sum[me])
        g.scalar.dma_start(T.y[:], T.land[:]).then_inc(T.sem.stored, 16)

    if step1[me]:
        g.wait_ge(T.sem.loaded, 16)
        g.remote_dma_fused(
            [RemoteDMATransfer(dst_ids=[dst_id(d)], dma_engine_mask=m, remote_sem=T.sem.raw,
                               srcs=[T.xs[s]], dsts=[place(d, me, s)], alu_op=0)
             for (d, s, n, m) in step1[me]],
            local_sem=T.sem.left)
    g.wait_ge(T.sem.raw, raw_sum[me])
    g.remote_dma_fused(
        [RemoteDMATransfer(dst_ids=[dst_id(r)], dma_engine_mask=m, remote_sem=T.sem.pre,
                           srcs=[place(me, i, s) for i in range(r)], dsts=[T.land[s]],
                           alu_op=2 if r > 1 else 0)
         for (r, s, n, m) in step2[me]],
        local_sem=T.sem.left)

    g.wait_ge(T.sem.left, left_sum[me])
    if me > 0:
        g.wait_ge(T.sem.stored, 16)
